import numpy as np
import ml_dtypes


def mxq(x, axis, fmt="e4m3"):
    dtype, down = {"e4m3": (ml_dtypes.float8_e4m3fn, 7), "e5m2": (ml_dtypes.float8_e5m2, 14)}[fmt]
    v = np.moveaxis(np.asarray(x, np.float32).astype(ml_dtypes.bfloat16).astype(np.float64), axis, -1)
    blocks = v.reshape(v.shape[:-1] + (-1, 32))
    amax = np.abs(blocks).max(-1, keepdims=True)
    byte = np.maximum(np.where(amax > 0, np.frexp(amax)[1] - 1 + 127, 0) - down, 1)
    scale = np.exp2(byte - 127.0)
    codes = (blocks / scale).astype(np.float32).astype(dtype).astype(np.float64)
    return np.moveaxis((codes * scale).reshape(v.shape), -1, axis)


WIDE = False


def mx_kscale(k):
    if not WIDE:
        return np.ones(k)
    levels = np.array([10, -10, 5, -5, 0])
    if k % 512:
        return np.exp2(np.random.permutation(np.resize(levels, k // 32))).repeat(32)
    a = np.empty((k // 512, 16))
    for p in range(k // 512):
        a[p, :8] = np.random.permutation(np.resize(levels, 8))
        for g in range(8):
            far = levels[np.abs(levels - a[p, g]) >= 10]
            a[p, g + 8] = far[np.random.randint(len(far))]
    return np.exp2(a.ravel()).repeat(32)


BF16 = ml_dtypes.bfloat16


def bf(x):
    return np.asarray(x, np.float32).astype(BF16)


def f64(x):
    return np.asarray(x).astype(np.float64)


E2M1 = np.array([0.0, 0.5, 1.0, 1.5, 2.0, 3.0, 4.0, 6.0, -0.0, -0.5, -1.0, -1.5, -2.0, -3.0, -4.0, -6.0])


def pack_weight(w, fmt):
    k, n = w.shape
    w = f64(bf(w)).reshape(k // 32, 32, n)
    amax = np.abs(w).max(1)
    if fmt == "e4m3":
        byte = np.frexp(amax)[1] - 1 + 127 - 7
    else:
        mant, ex = np.frexp(amax / 6.0)
        byte = np.where(mant > 0.5, ex, ex - 1) + 127
    byte = np.clip(np.where(amax > 0, byte, 1), 1, 254)
    scaled = (w * np.exp2(127.0 - byte)[:, None, :]).reshape(k, n).astype(np.float32)
    by_word = np.ascontiguousarray(scaled.reshape(k // 512, 128, 4, n).transpose(0, 1, 3, 2))
    if fmt == "e4m3":
        words = by_word.astype(ml_dtypes.float8_e4m3fn).view(np.uint8)
    else:
        c = by_word.astype(ml_dtypes.float4_e2m1fn).view(np.uint8) & 0xF
        words = c[..., 0::2] | (c[..., 1::2] << 4)
    return np.ascontiguousarray(words), np.ascontiguousarray(byte.astype(np.uint8).reshape(k // 512, 16, n))


def unpack_weight(words, scales, fmt):
    g, p, n, _ = words.shape
    if fmt == "e4m3":
        vals = np.ascontiguousarray(words).view(ml_dtypes.float8_e4m3fn).astype(np.float64)
    else:
        nib = np.empty((g, p, n, 4), np.uint8)
        nib[..., 0::2] = words & 0xF
        nib[..., 1::2] = words >> 4
        vals = E2M1[nib]
    vals = vals * np.repeat(np.exp2(scales.astype(np.float64) - 127.0), 8, axis=1)[..., None]
    return vals.transpose(0, 1, 3, 2).reshape(g * 512, n)
def pack4(w):
    words, scales = pack_weight(w, "e2m1")
    return words.reshape(words.shape[0], 128, -1), scales


def unpack4(words, scales):
    return unpack_weight(words.reshape(words.shape[0], 128, -1, 2), scales, "e2m1")


def planes(Y):
    n, m = Y.shape
    b = f64(bf(Y)).reshape(n // 32, 32, m)
    amax = np.abs(b).max(1)
    byte = np.clip(np.where(amax > 0, np.frexp(amax)[1] - 1 + 127 - 7, 1), 1, 254)
    codes = (b * np.exp2(127.0 - byte)[:, None, :]).reshape(n, m).astype(np.float32).astype(ml_dtypes.float8_e4m3fn).view(np.uint8)
    words = codes.reshape(n // 512, 128, 4, m).transpose(0, 1, 3, 2)
    return np.ascontiguousarray(words), np.ascontiguousarray(byte.astype(np.uint8).reshape(n // 512, 16, m))


M, D, F, N = 2048, 1536, 1024, 512

def setup_inputs():
    s = mx_kscale(D)
    t = mx_kscale(F)
    xt = np.random.randn(D, M) * s[:, None]
    x_words, x_scales = pack_weight(xt, "e4m3")
    w = np.random.randn(D, F) / np.sqrt(D) / s[:, None]
    w_words, w_scales = pack4(w)
    hidden_scale = bf(np.exp(0.3 * np.random.randn(F)) * t)
    code_matrix = bf(1.5 * np.random.randn(F, N) / np.sqrt(F) / t[:, None])
    bit_margin = bf(0.5 * np.exp(0.3 * np.random.randn(N)))
    bit_weight = bf(np.exp(0.8 * np.random.randn(N)))
    return {"x_words": x_words, "x_scales": x_scales, "w_words": w_words, "w_scales": w_scales,
            "hidden_scale": hidden_scale, "code_matrix": code_matrix,
            "bit_margin": bit_margin, "bit_weight": bit_weight}

def reference(x_words, x_scales, w_words, w_scales, hidden_scale, code_matrix, bit_margin, bit_weight):
    x = unpack_weight(x_words, x_scales, "e4m3").T
    w = unpack4(w_words, w_scales)
    h = np.tanh(x @ w) * f64(hidden_scale)
    z = mxq(h, 1, "e4m3") @ mxq(f64(code_matrix), 0, "e4m3")
    y = f64(bit_weight) * z / (f64(bit_margin) + np.abs(z))
    words, scales = planes(y.T)
    return y, words, scales

@@ -1,0 +1,331 @@
+from contextlib import ExitStack
+
+import concourse.mybir as mybir
+from concourse.masks import make_identity
+
+M, D, F, N = 2048, 1536, 1024, 512
+FLOPS = 2 * M * D * F + 2 * M * F * N
+
+F32 = mybir.dt.float32
+BF16 = mybir.dt.bfloat16
+I32 = mybir.dt.int32
+U32 = mybir.dt.uint32
+U8 = mybir.dt.uint8
+FP8X4 = mybir.dt.float8_e4m3fn_x4
+FP4X4 = mybir.dt.float4_e2m1fn_x4
+ACT = mybir.ActivationFunctionType
+ALU = mybir.AluOpType
+
+P = 128
+SLOTS = 4
+BANK = 512
+D_PASSES = D // (P * SLOTS)
+F_PASSES = F // (P * SLOTS)
+CHUNKS = M // BANK
+TILES = [(0, 512), (512, 512), (1024, 512), (1536, 256), (1792, 256)]
+VECTOR_SQUARES = [(0, 0), (0, 1), (0, 2), (0, 3), (1, 2), (1, 3)]
+SCALAR_COPIES = [(4, 0), (4, 1)]
+ACC_BANKS = 5
+TURN_BANKS = 3
+
+
+def tile_relaxed_document_hash_codes_h2_kernel(
+    tc, x_words, x_scales, w_words, w_scales, hidden_scale, code_matrix, bit_margin, bit_weight,
+    out_0, out_1, out_2,
+):
+    nc = tc.nc
+    with ExitStack() as ctx:
+        keep = ctx.enter_context(tc.tile_pool(name="keep", bufs=1))
+        work = ctx.enter_context(tc.tile_pool(name="work", bufs=3))
+        psum = ctx.enter_context(tc.psum_pool(name="psum", bufs=1))
+        ctx.enter_context(tc.manual_schedule())
+
+        def kept(name, shape, dtype):
+            return keep.tile(shape, dtype, name=name, align_bytes=64)
+
+        x_hbm = x_words.rearrange("g p m t -> p g (m t)").bitcast(I32)
+        xs_hbm = x_scales.rearrange("g r m -> r g m").bitcast(I32)
+        w_hbm = w_words.rearrange("g p b -> p g b").bitcast(I32)
+        ws_hbm = w_scales.rearrange("g r f -> r g f").bitcast(I32)
+
+        x_codes = [kept("x_codes%d" % c, [P, D_PASSES, BANK], U32) for c in range(CHUNKS)]
+        xs_first = kept("xs_first", [P, D_PASSES, BANK], U8)
+        xs_rest = kept("xs_rest", [P, D_PASSES, M - BANK], U8)
+        w_raw = [kept("w_raw%d" % g, [P, D_PASSES, 256], I32) for g in range(F_PASSES)]
+        w_codes = [kept("w_codes%d" % g, [P, D_PASSES, 1024], U8) for g in range(F_PASSES)]
+        ws_raw = kept("ws_raw", [P, D_PASSES, F], U8)
+        ws_plane = [kept("ws_plane%d" % g, [P, D_PASSES, BANK], U8) for g in range(F_PASSES)]
+        gain_rows = kept("gain_rows", [F_PASSES * SLOTS, P], BF16)
+        gain_square = kept("gain_square", [P, P], F32)
+        gain = kept("gain", [P, F_PASSES * SLOTS], F32)
+        ident = kept("ident", [P, P], F32)
+        c_raw = [kept("c_raw%d" % g, [P, SLOTS, N], BF16) for g in range(F_PASSES)]
+        c_words = [kept("c_words%d" % g, [P, N, SLOTS], BF16) for g in range(F_PASSES)]
+        c_codes = [kept("c_codes%d" % g, [P, N], U32) for g in range(F_PASSES)]
+        c_scales = [kept("c_scales%d" % g, [P, N], U8) for g in range(F_PASSES)]
+        h_codes = [kept("h_codes%d" % k, [P, BANK], U32) for k in range(CHUNKS * F_PASSES)]
+        h_scales = [kept("h_scales%d" % k, [P, BANK], U8) for k in range(CHUNKS * F_PASSES)]
+        margin = kept("margin", [P, SLOTS], BF16)
+        weight = kept("weight", [P, SLOTS], BF16)
+        inv_margin = kept("inv_margin", [P, SLOTS], F32)
+        factor = kept("factor", [P, SLOTS], F32)
+        y_codes = kept("y_codes", [P, M], U32)
+        y_scales = kept("y_scales", [P, M], U8)
+        warm = kept("warm", [P, 8], F32)
+
+        def load_scale_rows(plane, hbm, quad):
+            nc.sync.dma_start(out=plane[32 * quad : 32 * quad + 4].bitcast(I32), in_=hbm[4 * quad : 4 * quad + 4])
+
+        def load_x(c, engine):
+            engine.dma_start(out=x_codes[c][:].bitcast(I32), in_=x_hbm[:, :, c * BANK : (c + 1) * BANK])
+
+        def load_w(g, engine):
+            engine.dma_start(out=w_raw[g][:], in_=w_hbm[:, :, g * 256 : (g + 1) * 256])
+
+        def load_code_matrix(g):
+            rows = code_matrix[g * 512 : (g + 1) * 512, :].rearrange("(q t r) n -> r q t n", t=SLOTS, r=8)
+            for r in range(8):
+                nc.sync.dma_start(out=c_raw[g][r:P:8], in_=rows[r])
+
+        def order_w(g):
+            nc.vector.tensor_copy(
+                out=ws_plane[g][:].bitcast(I32).rearrange("p d (t q i) -> p d t q i", t=SLOTS, i=2),
+                in_=ws_raw[:, :, g * BANK : (g + 1) * BANK].bitcast(I32).rearrange("p d (q t i) -> p d t q i", t=SLOTS, i=2),
+            )
+            nc.vector.tensor_copy(
+                out=w_codes[g][:].bitcast(I32).rearrange("p d (t q i) -> p d t q i", t=SLOTS, i=4),
+                in_=w_raw[g][:].rearrange("p d (q t i) -> p d t q i", t=SLOTS, i=4),
+            )
+
+        nc.vector.memset(ws_raw[:].bitcast(I32), 0)
+        nc.vector.memset(xs_first[:].bitcast(I32), 0)
+        nc.vector.memset(xs_rest[:].bitcast(I32), 0)
+        load_scale_rows(ws_raw, ws_hbm, 0)
+        load_scale_rows(ws_raw, ws_hbm, 1)
+        load_x(0, nc.scalar)
+        load_w(0, nc.scalar)
+        load_scale_rows(ws_raw, ws_hbm, 2)
+        load_scale_rows(ws_raw, ws_hbm, 3)
+        for quad in range(4):
+            load_scale_rows(xs_first, xs_hbm[:, :, : BANK // 4], quad)
+        nc.gpsimd.memset(warm[:], 0.0)
+        nc.scalar.activation(out=warm[:, 4:5], in_=warm[:, 0:1], func=ACT.Tanh)
+        nc.gpsimd.memset(gain_square[:], 0.0)
+        make_identity(nc, ident[:])
+        load_w(1, nc.sync)
+        for g in range(F_PASSES):
+            nc.sync.dma_start(
+                out=gain_rows[g * SLOTS : (g + 1) * SLOTS, :].rearrange("t (q r) -> t q r", r=8),
+                in_=hidden_scale[g * 512 : (g + 1) * 512].rearrange("(q t r) -> t q r", t=SLOTS, r=8),
+            )
+        load_code_matrix(0)
+        for quad in range(4):
+            load_scale_rows(xs_rest, xs_hbm[:, :, BANK // 4 :], quad)
+        load_x(1, nc.sync)
+        load_code_matrix(1)
+        load_x(2, nc.sync)
+        load_x(3, nc.sync)
+        nc.sync.dma_start(out=margin[:], in_=bit_margin.rearrange("(p t) -> p t", t=SLOTS))
+        nc.sync.dma_start(out=weight[:], in_=bit_weight.rearrange("(p t) -> p t", t=SLOTS))
+
+        order_w(0)
+        nc.vector.tensor_copy(out=gain_square[0 : F_PASSES * SLOTS, :], in_=gain_rows[:])
+        order_w(1)
+
+        def x_scale_cols(c, d):
+            if c == 0:
+                return xs_first[:, d, :]
+            return xs_rest[:, d, (c - 1) * BANK : c * BANK]
+
+        def quantize_h(k):
+            nc.vector.quantize_mx(out=h_codes[k][:].bitcast(FP8X4), scales=h_scales[k][:], in_=h_words[k][:].rearrange("p m t -> p (m t)"))
+
+        def interleave_code_matrix(g, t):
+            nc.scalar.copy(
+                out=c_words[g][:, t * P : (t + 1) * P, :],
+                in_=c_raw[g][:].rearrange("p j (m t) -> p t m j", t=SLOTS)[:, t],
+            )
+
+        pieces = [(1, 1), (1, 3), (2, 1), (2, 3), (3, 1), (4, 1), (4, 3), (5, 1)]
+        h_words = {}
+        steps = CHUNKS * F_PASSES
+        for k in range(steps):
+            c, g = divmod(k, F_PASSES)
+            tanh = work.tile([P, SLOTS, BANK], F32, name="tanh", tag="tanh", bufs=3, align_bytes=64)
+            for t in range(SLOTS):
+                acc = psum.tile([P, BANK], F32, name="acc", tag="acc", bufs=ACC_BANKS)
+                for d in range(D_PASSES):
+                    nc.tensor.matmul_mx(
+                        out=acc[:],
+                        lhsT=w_codes[g][:, d, t * 256 : (t + 1) * 256].bitcast(FP4X4),
+                        lhsT_scale=ws_plane[g][:, d, t * P : (t + 1) * P],
+                        rhs=x_codes[c][:, d, :].bitcast(FP8X4),
+                        rhs_scale=x_scale_cols(c, d),
+                        start=(d == 0),
+                        stop=(d == D_PASSES - 1),
+                    )
+                nc.scalar.activation(out=tanh[:, t, :], in_=acc[:], func=ACT.Tanh)
+                if (k, t) in pieces:
+                    interleave_code_matrix(*divmod(pieces.index((k, t)), SLOTS))
+            if k == 0:
+                turned = psum.tile([P, BANK], F32, name="turned", tag="turned", bufs=TURN_BANKS)
+                nc.tensor.transpose(turned[:, 0:P], gain_square[:], ident[:])
+                nc.vector.tensor_copy(out=gain[:], in_=turned[:, 0 : F_PASSES * SLOTS])
+            if k in (3, 6):
+                cg = (3, 6).index(k)
+                nc.vector.quantize_mx(out=c_codes[cg][:].bitcast(FP8X4), scales=c_scales[cg][:], in_=c_words[cg][:].rearrange("p n t -> p (n t)"))
+            if k == 3:
+                nc.vector.reciprocal(out=inv_margin[:], in_=margin[:])
+            if k == 4:
+                nc.vector.tensor_tensor(out=factor[:], in0=weight[:], in1=inv_margin[:], op=ALU.mult)
+            h_words[k] = work.tile([P, BANK, SLOTS], BF16, name="h_words", tag="h_words", bufs=3, align_bytes=64)
+            nc.vector.tensor_tensor(
+                out=h_words[k][:].rearrange("p (a i) t -> p a t i", i=4),
+                in0=tanh[:].rearrange("p t (a i) -> p a t i", i=4),
+                in1=gain[:, g * SLOTS : (g + 1) * SLOTS].unsqueeze(1).unsqueeze(3).to_broadcast([P, BANK // 4, SLOTS, 4]),
+                op=ALU.mult,
+            )
+            if k > 0:
+                quantize_h(k - 1)
+        quantize_h(steps - 1)
+
+        slots = [(i, t) for i in range(len(TILES)) for t in range(SLOTS)]
+        last = len(TILES) - 1
+        z, mag, root, square, y, y_words, turned_out, staged = {}, {}, {}, {}, {}, {}, {}, {}
+        codes_hbm = out_1[0].rearrange("p m t -> p (m t)").bitcast(I32)
+        scales_hbm = out_2[0].bitcast(I32)
+
+        def logits(s):
+            i, t = slots[s]
+            first, width = TILES[i]
+            c, col = divmod(first, BANK)
+            z[s] = psum.tile([P, BANK], F32, name="acc", tag="acc", bufs=ACC_BANKS)
+            for g in range(F_PASSES):
+                k = c * F_PASSES + g
+                nc.tensor.matmul_mx(
+                    out=z[s][:, :width],
+                    lhsT=c_codes[g][:, t * P : (t + 1) * P].bitcast(FP8X4),
+                    lhsT_scale=c_scales[g][:, t * P : (t + 1) * P],
+                    rhs=h_codes[k][:, col : col + width].bitcast(FP8X4),
+                    rhs_scale=h_scales[k][:, col : col + width],
+                    start=(g == 0),
+                    stop=(g == F_PASSES - 1),
+                )
+
+        def magnitude(s):
+            i, t = slots[s]
+            width = TILES[i][1]
+            mag[s] = work.tile([P, width], F32, name="mag", tag="mag", bufs=3, align_bytes=64)
+            nc.scalar.activation(out=mag[s][:], in_=z[s][:, :width], func=ACT.Abs, scale=inv_margin[:, t : t + 1])
+
+        def inverse_root(s):
+            width = TILES[slots[s][0]][1]
+            root[s] = work.tile([P, width], F32, name="root", tag="root", bufs=4, align_bytes=64)
+            nc.scalar.activation(out=root[s][:], in_=mag[s][:], func=ACT.Abs_reciprocal_sqrt, bias=1.0)
+
+        def scalar_square(s):
+            width = TILES[slots[s][0]][1]
+            square[s] = work.tile([P, width], F32, name="square", tag="square", bufs=4, align_bytes=64)
+            if slots[s] not in VECTOR_SQUARES:
+                nc.scalar.activation(out=square[s][:], in_=root[s][:], func=ACT.Square)
+
+        def product(s):
+            i, t = slots[s]
+            width = TILES[i][1]
+            if t == 0:
+                y[i] = work.tile([P, SLOTS, width], F32, name="y", tag="y", bufs=3, align_bytes=64)
+            on_vector = slots[s] in VECTOR_SQUARES
+            nc.vector.scalar_tensor_tensor(
+                out=square[s][:] if on_vector else y[i][:, t, :],
+                in0=z[s][:, :width],
+                scalar=factor[:, t : t + 1],
+                in1=root[s][:] if on_vector else square[s][:],
+                op0=ALU.mult,
+                op1=ALU.mult,
+            )
+
+        def second_product(s):
+            i, t = slots[s]
+            if slots[s] in VECTOR_SQUARES:
+                nc.vector.tensor_tensor(out=y[i][:, t, :], in0=square[s][:], in1=root[s][:], op=ALU.mult)
+
+        def round_y(i):
+            width = TILES[i][1]
+            y_words[i] = work.tile([P, width, SLOTS], BF16, name="y_words", tag="y_words", bufs=2, align_bytes=64)
+            if i < last:
+                nc.gpsimd.tensor_scalar(
+                    out=y_words[i][:], in0=y[i][:].rearrange("p t m -> p m t"),
+                    scalar1=1.0, scalar2=-0.0, op0=ALU.mult, op1=ALU.add,
+                )
+            else:
+                nc.vector.tensor_copy(
+                    out=y_words[i][:].rearrange("p (a i) t -> p a t i", i=4),
+                    in_=y[i][:].rearrange("p t (a i) -> p a t i", i=4),
+                )
+
+        def quantize_y(i):
+            first, width = TILES[i]
+            cols = slice(first, first + width)
+            nc.vector.quantize_mx(out=y_codes[:, cols].bitcast(FP8X4), scales=y_scales[:, cols], in_=y_words[i][:].rearrange("p m t -> p (m t)"))
+            nc.sync.dma_start(out=codes_hbm[:, cols], in_=y_codes[:, cols].bitcast(I32))
+
+        def store_scales(first, end, engines):
+            cols = slice(first // 4, end // 4)
+            for quad in range(4):
+                engines[quad % len(engines)].dma_start(
+                    out=scales_hbm[4 * quad : 4 * quad + 4, cols],
+                    in_=y_scales[32 * quad : 32 * quad + 4, :].bitcast(I32)[:, cols],
+                )
+
+        def turn(i, j):
+            turned_out[i, j] = psum.tile([P, BANK], F32, name="turned", tag="turned", bufs=TURN_BANKS)
+            for t in range(SLOTS):
+                nc.tensor.transpose(turned_out[i, j][:, t * P : (t + 1) * P], y[i][:, t, j * P : (j + 1) * P], ident[:])
+
+        def copy_out(i, j):
+            first, width = TILES[i]
+            rows = work.tile([P, N], F32, name="rows", tag="rows", bufs=6, align_bytes=64)
+            target = rows[:].rearrange("p (b t) -> p b t", t=SLOTS)
+            source = turned_out[i, j][:].rearrange("p (t b) -> p b t", t=SLOTS)
+            if (i, j) in SCALAR_COPIES:
+                nc.scalar.copy(out=target, in_=source)
+            else:
+                nc.vector.tensor_copy(out=target, in_=source)
+            nc.sync.dma_start(out=out_0[first + j * P : first + (j + 1) * P, :], in_=rows[:])
+            if j + TURN_BANKS < width // P:
+                turn(i, j + TURN_BANKS)
+
+        for s in range(ACC_BANKS):
+            logits(s)
+        for tick in range(len(slots) + 2):
+            if tick < len(slots):
+                magnitude(tick)
+            if 1 <= tick <= len(slots):
+                inverse_root(tick - 1)
+            if tick < 2:
+                continue
+            s = tick - 2
+            i, t = slots[s]
+            scalar_square(s)
+            if i > 0 and t == 3:
+                quantize_y(i - 1)
+                if i == last:
+                    store_scales(0, TILES[last][0], [nc.sync])
+            product(s)
+            if s + ACC_BANKS < len(slots):
+                logits(s + ACC_BANKS)
+            if i > 0 and t < TILES[i - 1][1] // P:
+                copy_out(i - 1, t)
+            if i == 0 and t > 0:
+                second_product(s - 1)
+            if i > 0 or t == SLOTS - 1:
+                second_product(s)
+            if t == SLOTS - 1:
+                round_y(i)
+                for j in range(min(TURN_BANKS, TILES[i][1] // P)):
+                    turn(i, j)
+        for j in range(TILES[last][1] // P):
+            copy_out(last, j)
+            if j == 0:
+                quantize_y(last)
+        store_scales(TILES[last][0], M, [nc.scalar, nc.sync])

@@ -22,9 +22,11 @@ BANK = 512
 D_PASSES = D // (P * SLOTS)
 F_PASSES = F // (P * SLOTS)
 CHUNKS = M // BANK
-TILES = [(0, 512), (512, 512), (1024, 512), (1536, 256), (1792, 256)]
-VECTOR_SQUARES = [(0, 0), (0, 1), (0, 2), (0, 3), (1, 2), (1, 3)]
-SCALAR_COPIES = [(4, 0), (4, 1)]
+WIDTHS = [256]*8
+VECTOR_SQUARES = [0,1,3,5,7,9]
+POOL_SQUARES = []
+LAG = 2
+SCALAR_COPIES = [13,14,15]
 ACC_BANKS = 5
 TURN_BANKS = 3
 
@@ -67,11 +69,10 @@ def tile_relaxed_document_hash_codes_h2_kernel(
         h_scales = [kept("h_scales%d" % k, [P, BANK], U8) for k in range(CHUNKS * F_PASSES)]
         margin = kept("margin", [P, SLOTS], BF16)
         weight = kept("weight", [P, SLOTS], BF16)
-        inv_margin = kept("inv_margin", [P, SLOTS], F32)
-        factor = kept("factor", [P, SLOTS], F32)
+        inv_weight = kept("inv_weight", [P, SLOTS], F32)
+        offset = kept("offset", [P, SLOTS], F32)
         y_codes = kept("y_codes", [P, M], U32)
         y_scales = kept("y_scales", [P, M], U8)
-        warm = kept("warm", [P, 8], F32)
 
         def load_scale_rows(plane, hbm, quad):
             nc.sync.dma_start(out=plane[32 * quad : 32 * quad + 4].bitcast(I32), in_=hbm[4 * quad : 4 * quad + 4])
@@ -88,28 +89,27 @@ def tile_relaxed_document_hash_codes_h2_kernel(
                 nc.sync.dma_start(out=c_raw[g][r:P:8], in_=rows[r])
 
         def order_w(g):
-            nc.vector.tensor_copy(
-                out=ws_plane[g][:].bitcast(I32).rearrange("p d (t q i) -> p d t q i", t=SLOTS, i=2),
-                in_=ws_raw[:, :, g * BANK : (g + 1) * BANK].bitcast(I32).rearrange("p d (q t i) -> p d t q i", t=SLOTS, i=2),
-            )
+            for quad in range(4):
+                live = slice(32 * quad, 32 * quad + 4)
+                nc.vector.tensor_copy(
+                    out=ws_plane[g][live].bitcast(I32).rearrange("p d (t q i) -> p d t q i", t=SLOTS, i=2),
+                    in_=ws_raw[live, :, g * BANK : (g + 1) * BANK].bitcast(I32).rearrange("p d (q t i) -> p d t q i", t=SLOTS, i=2),
+                )
             nc.vector.tensor_copy(
                 out=w_codes[g][:].bitcast(I32).rearrange("p d (t q i) -> p d t q i", t=SLOTS, i=4),
                 in_=w_raw[g][:].rearrange("p d (q t i) -> p d t q i", t=SLOTS, i=4),
             )
 
-        nc.vector.memset(ws_raw[:].bitcast(I32), 0)
-        nc.vector.memset(xs_first[:].bitcast(I32), 0)
-        nc.vector.memset(xs_rest[:].bitcast(I32), 0)
-        load_scale_rows(ws_raw, ws_hbm, 0)
-        load_scale_rows(ws_raw, ws_hbm, 1)
-        load_x(0, nc.scalar)
+        for quad in range(4):
+            load_scale_rows(ws_raw, ws_hbm, quad)
         load_w(0, nc.scalar)
-        load_scale_rows(ws_raw, ws_hbm, 2)
-        load_scale_rows(ws_raw, ws_hbm, 3)
+        load_x(0, nc.scalar)
+        nc.vector.memset(xs_first[:].bitcast(I32), 0)
         for quad in range(4):
             load_scale_rows(xs_first, xs_hbm[:, :, : BANK // 4], quad)
-        nc.gpsimd.memset(warm[:], 0.0)
-        nc.scalar.activation(out=warm[:, 4:5], in_=warm[:, 0:1], func=ACT.Tanh)
+        for g in range(F_PASSES):
+            nc.vector.memset(ws_plane[g][:].bitcast(I32), 0)
+        nc.vector.memset(xs_rest[:].bitcast(I32), 0)
         nc.gpsimd.memset(gain_square[:], 0.0)
         make_identity(nc, ident[:])
         load_w(1, nc.sync)
@@ -118,10 +118,10 @@ def tile_relaxed_document_hash_codes_h2_kernel(
                 out=gain_rows[g * SLOTS : (g + 1) * SLOTS, :].rearrange("t (q r) -> t q r", r=8),
                 in_=hidden_scale[g * 512 : (g + 1) * 512].rearrange("(q t r) -> t q r", t=SLOTS, r=8),
             )
-        load_code_matrix(0)
         for quad in range(4):
             load_scale_rows(xs_rest, xs_hbm[:, :, BANK // 4 :], quad)
         load_x(1, nc.sync)
+        load_code_matrix(0)
         load_code_matrix(1)
         load_x(2, nc.sync)
         load_x(3, nc.sync)
@@ -146,7 +146,7 @@ def tile_relaxed_document_hash_codes_h2_kernel(
                 in_=c_raw[g][:].rearrange("p j (m t) -> p t m j", t=SLOTS)[:, t],
             )
 
-        pieces = [(1, 1), (1, 3), (2, 1), (2, 3), (3, 1), (4, 1), (4, 3), (5, 1)]
+        pieces = [(2, 1), (3, 1), (4, 1), (5, 1)]
         h_words = {}
         steps = CHUNKS * F_PASSES
         for k in range(steps):
@@ -166,18 +166,23 @@ def tile_relaxed_document_hash_codes_h2_kernel(
                     )
                 nc.scalar.activation(out=tanh[:, t, :], in_=acc[:], func=ACT.Tanh)
                 if (k, t) in pieces:
-                    interleave_code_matrix(*divmod(pieces.index((k, t)), SLOTS))
+                    interleave_code_matrix(1, pieces.index((k, t)))
             if k == 0:
                 turned = psum.tile([P, BANK], F32, name="turned", tag="turned", bufs=TURN_BANKS)
                 nc.tensor.transpose(turned[:, 0:P], gain_square[:], ident[:])
                 nc.vector.tensor_copy(out=gain[:], in_=turned[:, 0 : F_PASSES * SLOTS])
-            if k in (3, 6):
-                cg = (3, 6).index(k)
+            if k in (2, 6):
+                cg = (2, 6).index(k)
                 nc.vector.quantize_mx(out=c_codes[cg][:].bitcast(FP8X4), scales=c_scales[cg][:], in_=c_words[cg][:].rearrange("p n t -> p (n t)"))
+            if k == 1:
+                nc.vector.tensor_copy(
+                    out=c_words[0][:].rearrange("p (t m) j -> p t m j", t=SLOTS),
+                    in_=c_raw[0][:].rearrange("p j (m t) -> p t m j", t=SLOTS),
+                )
             if k == 3:
-                nc.vector.reciprocal(out=inv_margin[:], in_=margin[:])
+                nc.vector.reciprocal(out=inv_weight[:], in_=weight[:])
             if k == 4:
-                nc.vector.tensor_tensor(out=factor[:], in0=weight[:], in1=inv_margin[:], op=ALU.mult)
+                nc.vector.tensor_tensor(out=offset[:], in0=margin[:], in1=inv_weight[:], op=ALU.mult)
             h_words[k] = work.tile([P, BANK, SLOTS], BF16, name="h_words", tag="h_words", bufs=3, align_bytes=64)
             nc.vector.tensor_tensor(
                 out=h_words[k][:].rearrange("p (a i) t -> p a t i", i=4),
@@ -189,69 +194,76 @@ def tile_relaxed_document_hash_codes_h2_kernel(
                 quantize_h(k - 1)
         quantize_h(steps - 1)
 
-        slots = [(i, t) for i in range(len(TILES)) for t in range(SLOTS)]
-        last = len(TILES) - 1
-        z, mag, root, square, y, y_words, turned_out, staged = {}, {}, {}, {}, {}, {}, {}, {}
+        firsts = [sum(WIDTHS[:i]) for i in range(len(WIDTHS))]
+        banks = [(i, j) for i, width in enumerate(WIDTHS) for j in range(width // P)]
+        last = len(WIDTHS) - 1
+        z, mag, root, square, y, y_words, turned_out = {}, {}, {}, {}, {}, {}, {}
         codes_hbm = out_1[0].rearrange("p m t -> p (m t)").bitcast(I32)
         scales_hbm = out_2[0].bitcast(I32)
 
-        def logits(s):
-            i, t = slots[s]
-            first, width = TILES[i]
-            c, col = divmod(first, BANK)
-            z[s] = psum.tile([P, BANK], F32, name="acc", tag="acc", bufs=ACC_BANKS)
-            for g in range(F_PASSES):
-                k = c * F_PASSES + g
-                nc.tensor.matmul_mx(
-                    out=z[s][:, :width],
-                    lhsT=c_codes[g][:, t * P : (t + 1) * P].bitcast(FP8X4),
-                    lhsT_scale=c_scales[g][:, t * P : (t + 1) * P],
-                    rhs=h_codes[k][:, col : col + width].bitcast(FP8X4),
-                    rhs_scale=h_scales[k][:, col : col + width],
-                    start=(g == 0),
-                    stop=(g == F_PASSES - 1),
+        def slots_of(b):
+            i, j = banks[b]
+            count = BANK // WIDTHS[i]
+            return range(j * count, (j + 1) * count)
+
+        def y_part(b):
+            slots = slots_of(b)
+            return y[banks[b][0]][:, slots.start : slots.stop, :].rearrange("p t m -> p (t m)")
+
+        def logits(b):
+            i = banks[b][0]
+            width = WIDTHS[i]
+            c, col = divmod(firsts[i], BANK)
+            z[b] = psum.tile([P, BANK], F32, name="acc", tag="acc", bufs=ACC_BANKS)
+            for n, t in enumerate(slots_of(b)):
+                for g in range(F_PASSES):
+                    k = c * F_PASSES + g
+                    nc.tensor.matmul_mx(
+                        out=z[b][:, n * width : (n + 1) * width],
+                        lhsT=c_codes[g][:, t * P : (t + 1) * P].bitcast(FP8X4),
+                        lhsT_scale=c_scales[g][:, t * P : (t + 1) * P],
+                        rhs=h_codes[k][:, col : col + width].bitcast(FP8X4),
+                        rhs_scale=h_scales[k][:, col : col + width],
+                        start=(g == 0),
+                        stop=(g == F_PASSES - 1),
+                    )
+
+        def magnitude(b):
+            mag[b] = work.tile([P, BANK], F32, name="mag", tag="mag", bufs=3, align_bytes=64)
+            nc.scalar.activation(out=mag[b][:], in_=z[b][:], func=ACT.Abs)
+
+        def inverse_root(b):
+            width = WIDTHS[banks[b][0]]
+            root[b] = work.tile([P, BANK], F32, name="root", tag="root", bufs=5, align_bytes=64)
+            for n, t in enumerate(slots_of(b)):
+                cols = slice(n * width, (n + 1) * width)
+                nc.scalar.activation(
+                    out=root[b][:, cols], in_=mag[b][:, cols], func=ACT.Abs_reciprocal_sqrt,
+                    scale=inv_weight[:, t : t + 1], bias=offset[:, t : t + 1],
                 )
 
-        def magnitude(s):
-            i, t = slots[s]
-            width = TILES[i][1]
-            mag[s] = work.tile([P, width], F32, name="mag", tag="mag", bufs=3, align_bytes=64)
-            nc.scalar.activation(out=mag[s][:], in_=z[s][:, :width], func=ACT.Abs, scale=inv_margin[:, t : t + 1])
+        def square_root(b):
+            square[b] = work.tile([P, BANK], F32, name="square", tag="square", bufs=5, align_bytes=64)
+            if b in POOL_SQUARES:
+                nc.gpsimd.tensor_tensor(out=square[b][:], in0=root[b][:], in1=root[b][:], op=ALU.mult)
+            elif b not in VECTOR_SQUARES:
+                nc.scalar.activation(out=square[b][:], in_=root[b][:], func=ACT.Square)
 
-        def inverse_root(s):
-            width = TILES[slots[s][0]][1]
-            root[s] = work.tile([P, width], F32, name="root", tag="root", bufs=4, align_bytes=64)
-            nc.scalar.activation(out=root[s][:], in_=mag[s][:], func=ACT.Abs_reciprocal_sqrt, bias=1.0)
+        def product(b):
+            i, j = banks[b]
+            if j == 0:
+                y[i] = work.tile([P, SLOTS, WIDTHS[i]], F32, name="y", tag="y", bufs=4, align_bytes=64)
+            if b in VECTOR_SQUARES:
+                nc.vector.tensor_tensor(out=square[b][:], in0=z[b][:], in1=root[b][:], op=ALU.mult)
+            else:
+                nc.vector.tensor_tensor(out=y_part(b), in0=z[b][:], in1=square[b][:], op=ALU.mult)
 
-        def scalar_square(s):
-            width = TILES[slots[s][0]][1]
-            square[s] = work.tile([P, width], F32, name="square", tag="square", bufs=4, align_bytes=64)
-            if slots[s] not in VECTOR_SQUARES:
-                nc.scalar.activation(out=square[s][:], in_=root[s][:], func=ACT.Square)
-
-        def product(s):
-            i, t = slots[s]
-            width = TILES[i][1]
-            if t == 0:
-                y[i] = work.tile([P, SLOTS, width], F32, name="y", tag="y", bufs=3, align_bytes=64)
-            on_vector = slots[s] in VECTOR_SQUARES
-            nc.vector.scalar_tensor_tensor(
-                out=square[s][:] if on_vector else y[i][:, t, :],
-                in0=z[s][:, :width],
-                scalar=factor[:, t : t + 1],
-                in1=root[s][:] if on_vector else square[s][:],
-                op0=ALU.mult,
-                op1=ALU.mult,
-            )
-
-        def second_product(s):
-            i, t = slots[s]
-            if slots[s] in VECTOR_SQUARES:
-                nc.vector.tensor_tensor(out=y[i][:, t, :], in0=square[s][:], in1=root[s][:], op=ALU.mult)
+        def second_product(b):
+            if b in VECTOR_SQUARES:
+                nc.vector.tensor_tensor(out=y_part(b), in0=square[b][:], in1=root[b][:], op=ALU.mult)
 
         def round_y(i):
-            width = TILES[i][1]
-            y_words[i] = work.tile([P, width, SLOTS], BF16, name="y_words", tag="y_words", bufs=2, align_bytes=64)
+            y_words[i] = work.tile([P, WIDTHS[i], SLOTS], BF16, name="y_words", tag="y_words", bufs=4, align_bytes=64)
             if i < last:
                 nc.gpsimd.tensor_scalar(
                     out=y_words[i][:], in0=y[i][:].rearrange("p t m -> p m t"),
@@ -264,68 +276,87 @@ def tile_relaxed_document_hash_codes_h2_kernel(
                 )
 
         def quantize_y(i):
-            first, width = TILES[i]
-            cols = slice(first, first + width)
+            cols = slice(firsts[i], firsts[i] + WIDTHS[i])
             nc.vector.quantize_mx(out=y_codes[:, cols].bitcast(FP8X4), scales=y_scales[:, cols], in_=y_words[i][:].rearrange("p m t -> p (m t)"))
-            nc.sync.dma_start(out=codes_hbm[:, cols], in_=y_codes[:, cols].bitcast(I32))
 
-        def store_scales(first, end, engines):
+            end = cols.stop
+            if end % BANK == 0:
+                nc.sync.dma_start(out=codes_hbm[:, end - BANK : end], in_=y_codes[:, end - BANK : end].bitcast(I32))
+            if end == 1024:
+                store_scales(0, end)
+            if end == M:
+                store_scales(1024, M)
+
+        def store_scales(first, end):
             cols = slice(first // 4, end // 4)
             for quad in range(4):
-                engines[quad % len(engines)].dma_start(
+                nc.sync.dma_start(
                     out=scales_hbm[4 * quad : 4 * quad + 4, cols],
                     in_=y_scales[32 * quad : 32 * quad + 4, :].bitcast(I32)[:, cols],
                 )
 
-        def turn(i, j):
-            turned_out[i, j] = psum.tile([P, BANK], F32, name="turned", tag="turned", bufs=TURN_BANKS)
+        def turn(b):
+            i, j = banks[b]
+            turned_out[b] = psum.tile([P, BANK], F32, name="turned", tag="turned", bufs=TURN_BANKS)
             for t in range(SLOTS):
-                nc.tensor.transpose(turned_out[i, j][:, t * P : (t + 1) * P], y[i][:, t, j * P : (j + 1) * P], ident[:])
+                nc.tensor.transpose(turned_out[b][:, t * P : (t + 1) * P], y[i][:, t, j * P : (j + 1) * P], ident[:])
 
-        def copy_out(i, j):
-            first, width = TILES[i]
+        def copy_out(b):
             rows = work.tile([P, N], F32, name="rows", tag="rows", bufs=6, align_bytes=64)
-            target = rows[:].rearrange("p (b t) -> p b t", t=SLOTS)
-            source = turned_out[i, j][:].rearrange("p (t b) -> p b t", t=SLOTS)
-            if (i, j) in SCALAR_COPIES:
+            target = rows[:].rearrange("p (n t) -> p n t", t=SLOTS)
+            source = turned_out[b][:].rearrange("p (t n) -> p n t", t=SLOTS)
+            if b in SCALAR_COPIES:
                 nc.scalar.copy(out=target, in_=source)
             else:
                 nc.vector.tensor_copy(out=target, in_=source)
-            nc.sync.dma_start(out=out_0[first + j * P : first + (j + 1) * P, :], in_=rows[:])
-            if j + TURN_BANKS < width // P:
-                turn(i, j + TURN_BANKS)
+            nc.sync.dma_start(out=out_0[b * P : (b + 1) * P, :], in_=rows[:])
 
-        for s in range(ACC_BANKS):
-            logits(s)
-        for tick in range(len(slots) + 2):
-            if tick < len(slots):
+        for b in range(ACC_BANKS):
+            logits(b)
+        to_turn, to_copy, to_quantize = [], [], []
+
+        def turn_ready():
+            while to_turn and len(to_copy) < TURN_BANKS:
+                turn(to_turn[0])
+                to_copy.append(to_turn[0])
+                to_turn.remove(to_turn[0])
+
+        def copy_next():
+            copy_out(to_copy[0])
+            to_copy.remove(to_copy[0])
+            turn_ready()
+
+        for tick in range(len(banks) + LAG):
+            if tick < len(banks):
                 magnitude(tick)
-            if 1 <= tick <= len(slots):
+            if 1 <= tick <= len(banks):
                 inverse_root(tick - 1)
-            if tick < 2:
+                if tick - 1 in POOL_SQUARES:
+                    square_root(tick - 1)
+            if 2 <= tick < len(banks) + 2 and tick - 2 not in POOL_SQUARES:
+                square_root(tick - 2)
+            if tick < LAG:
                 continue
-            s = tick - 2
-            i, t = slots[s]
-            scalar_square(s)
-            if i > 0 and t == 3:
-                quantize_y(i - 1)
+            b = tick - LAG
+            i, j = banks[b]
+            finishes = j == WIDTHS[i] // P - 1
+            if finishes and i >= 2 and b not in VECTOR_SQUARES:
+                quantize_y(i - 2)
+            product(b)
+            if b + ACC_BANKS < len(banks):
+                logits(b + ACC_BANKS)
+            if to_copy:
+                copy_next()
+            if finishes and i >= 2 and b in VECTOR_SQUARES:
+                quantize_y(i - 2)
+            second_product(b)
+            if finishes:
                 if i == last:
-                    store_scales(0, TILES[last][0], [nc.sync])
-            product(s)
-            if s + ACC_BANKS < len(slots):
-                logits(s + ACC_BANKS)
-            if i > 0 and t < TILES[i - 1][1] // P:
-                copy_out(i - 1, t)
-            if i == 0 and t > 0:
-                second_product(s - 1)
-            if i > 0 or t == SLOTS - 1:
-                second_product(s)
-            if t == SLOTS - 1:
+                    for done in range(last - 2 + 1, last):
+                        quantize_y(done)
                 round_y(i)
-                for j in range(min(TURN_BANKS, TILES[i][1] // P)):
-                    turn(i, j)
-        for j in range(TILES[last][1] // P):
-            copy_out(last, j)
-            if j == 0:
-                quantize_y(last)
-        store_scales(TILES[last][0], M, [nc.scalar, nc.sync])
+                to_turn.extend(range(b - j, b + 1))
+                turn_ready()
+        while to_copy:
+            copy_next()
+        quantize_y(last)

@@ -18,17 +18,23 @@ ALU = mybir.AluOpType
 
 P = 128
 SLOTS = 4
+PASS = P * SLOTS
 BANK = 512
-D_PASSES = D // (P * SLOTS)
-F_PASSES = F // (P * SLOTS)
+QUADS = 4
+RUN = 8
+D_PASSES = D // PASS
+F_PASSES = F // PASS
 CHUNKS = M // BANK
-WIDTHS = [256]*8
-VECTOR_SQUARES = [0,1,3,5,7,9]
-POOL_SQUARES = []
+STEPS = CHUNKS * F_PASSES
+TILE = 256
+TILES = M // TILE
+PAIRS = 2 * TILES
+
+SUM_BANKS = 6
+TURN_BANKS = 2
+VECTOR_SQUARES = 4
+SCALAR_COPIES = 4
 LAG = 2
-SCALAR_COPIES = [13,14,15]
-ACC_BANKS = 5
-TURN_BANKS = 3
 
 
 def tile_relaxed_document_hash_codes_h2_kernel(
@@ -45,18 +51,35 @@ def tile_relaxed_document_hash_codes_h2_kernel(
         def kept(name, shape, dtype):
             return keep.tile(shape, dtype, name=name, align_bytes=64)
 
-        x_hbm = x_words.rearrange("g p m t -> p g (m t)").bitcast(I32)
-        xs_hbm = x_scales.rearrange("g r m -> r g m").bitcast(I32)
-        w_hbm = w_words.rearrange("g p b -> p g b").bitcast(I32)
-        ws_hbm = w_scales.rearrange("g r f -> r g f").bitcast(I32)
+        def streamed(name, shape, dtype, bufs):
+            return work.tile(shape, dtype, name=name, tag=name, bufs=bufs, align_bytes=64)
 
-        x_codes = [kept("x_codes%d" % c, [P, D_PASSES, BANK], U32) for c in range(CHUNKS)]
+        def sum_bank():
+            return psum.tile([P, BANK], F32, name="sums", tag="sums", bufs=SUM_BANKS)
+
+        def turn_bank():
+            return psum.tile([P, BANK], F32, name="turned", tag="turned", bufs=TURN_BANKS)
+
+        def quantize(codes, scales, words):
+            nc.vector.quantize_mx(
+                out=codes.bitcast(FP8X4), scales=scales, in_=words.rearrange("p c t -> p (c t)")
+            )
+
+        x_hbm = x_words.rearrange("d p m t -> p d (m t)").bitcast(I32)
+        xs_hbm = x_scales.rearrange("d r m -> r d m").bitcast(I32)
+        w_hbm = w_words.rearrange("d p b -> p d b").bitcast(I32)
+        ws_hbm = w_scales.rearrange("d r f -> r d f").bitcast(I32)
+        codes_hbm = out_1[0].rearrange("p m t -> p (m t)").bitcast(I32)
+        scales_hbm = out_2[0].bitcast(I32)
+
+        x_first = [kept("x_first%d" % d, [P, BANK], U32) for d in range(D_PASSES)]
+        x_rest = [kept("x_rest%d" % c, [P, D_PASSES, BANK], U32) for c in range(1, CHUNKS)]
         xs_first = kept("xs_first", [P, D_PASSES, BANK], U8)
         xs_rest = kept("xs_rest", [P, D_PASSES, M - BANK], U8)
-        w_raw = [kept("w_raw%d" % g, [P, D_PASSES, 256], I32) for g in range(F_PASSES)]
-        w_codes = [kept("w_codes%d" % g, [P, D_PASSES, 1024], U8) for g in range(F_PASSES)]
+        w_raw = [kept("w_raw%d" % g, [P, D_PASSES, PASS // 2], I32) for g in range(F_PASSES)]
+        w_codes = [kept("w_codes%d" % g, [P, D_PASSES, 2 * PASS], U8) for g in range(F_PASSES)]
         ws_raw = kept("ws_raw", [P, D_PASSES, F], U8)
-        ws_plane = [kept("ws_plane%d" % g, [P, D_PASSES, BANK], U8) for g in range(F_PASSES)]
+        ws_plane = [kept("ws_plane%d" % g, [P, D_PASSES, PASS], U8) for g in range(F_PASSES)]
         gain_rows = kept("gain_rows", [F_PASSES * SLOTS, P], BF16)
         gain_square = kept("gain_square", [P, P], F32)
         gain = kept("gain", [P, F_PASSES * SLOTS], F32)
@@ -65,8 +88,8 @@ def tile_relaxed_document_hash_codes_h2_kernel(
         c_words = [kept("c_words%d" % g, [P, N, SLOTS], BF16) for g in range(F_PASSES)]
         c_codes = [kept("c_codes%d" % g, [P, N], U32) for g in range(F_PASSES)]
         c_scales = [kept("c_scales%d" % g, [P, N], U8) for g in range(F_PASSES)]
-        h_codes = [kept("h_codes%d" % k, [P, BANK], U32) for k in range(CHUNKS * F_PASSES)]
-        h_scales = [kept("h_scales%d" % k, [P, BANK], U8) for k in range(CHUNKS * F_PASSES)]
+        h_codes = [kept("h_codes%d" % k, [P, BANK], U32) for k in range(STEPS)]
+        h_scales = [kept("h_scales%d" % k, [P, BANK], U8) for k in range(STEPS)]
         margin = kept("margin", [P, SLOTS], BF16)
         weight = kept("weight", [P, SLOTS], BF16)
         inv_weight = kept("inv_weight", [P, SLOTS], F32)
@@ -74,39 +97,45 @@ def tile_relaxed_document_hash_codes_h2_kernel(
         y_codes = kept("y_codes", [P, M], U32)
         y_scales = kept("y_scales", [P, M], U8)
 
-        def load_scale_rows(plane, hbm, quad):
-            nc.sync.dma_start(out=plane[32 * quad : 32 * quad + 4].bitcast(I32), in_=hbm[4 * quad : 4 * quad + 4])
+        def scale_rows(quad):
+            return slice(32 * quad, 32 * quad + 4)
 
-        def load_x(c, engine):
-            engine.dma_start(out=x_codes[c][:].bitcast(I32), in_=x_hbm[:, :, c * BANK : (c + 1) * BANK])
+        def load_scales(plane, hbm):
+            for quad in range(QUADS):
+                nc.sync.dma_start(out=plane[scale_rows(quad)].bitcast(I32), in_=hbm[4 * quad : 4 * quad + 4])
 
-        def load_w(g, engine):
-            engine.dma_start(out=w_raw[g][:], in_=w_hbm[:, :, g * 256 : (g + 1) * 256])
+        def load_w(g, queue):
+            queue.dma_start(out=w_raw[g][:], in_=w_hbm[:, :, g * PASS // 2 : (g + 1) * PASS // 2])
+
+        def load_x(c):
+            nc.sync.dma_start(out=x_rest[c - 1][:].bitcast(I32), in_=x_hbm[:, :, c * BANK : (c + 1) * BANK])
 
         def load_code_matrix(g):
-            rows = code_matrix[g * 512 : (g + 1) * 512, :].rearrange("(q t r) n -> r q t n", t=SLOTS, r=8)
-            for r in range(8):
-                nc.sync.dma_start(out=c_raw[g][r:P:8], in_=rows[r])
+            rows = code_matrix[g * PASS : (g + 1) * PASS, :].rearrange("(q t r) n -> r q t n", t=SLOTS, r=RUN)
+            for r in range(RUN):
+                nc.sync.dma_start(out=c_raw[g][r:P:RUN], in_=rows[r])
 
         def order_w(g):
-            for quad in range(4):
-                live = slice(32 * quad, 32 * quad + 4)
+            for quad in range(QUADS):
+                rows = scale_rows(quad)
                 nc.vector.tensor_copy(
-                    out=ws_plane[g][live].bitcast(I32).rearrange("p d (t q i) -> p d t q i", t=SLOTS, i=2),
-                    in_=ws_raw[live, :, g * BANK : (g + 1) * BANK].bitcast(I32).rearrange("p d (q t i) -> p d t q i", t=SLOTS, i=2),
+                    out=ws_plane[g][rows].bitcast(I32).rearrange("p d (t q i) -> p d t q i", t=SLOTS, i=2),
+                    in_=ws_raw[rows, :, g * PASS : (g + 1) * PASS]
+                    .bitcast(I32)
+                    .rearrange("p d (q t i) -> p d t q i", t=SLOTS, i=2),
                 )
             nc.vector.tensor_copy(
                 out=w_codes[g][:].bitcast(I32).rearrange("p d (t q i) -> p d t q i", t=SLOTS, i=4),
                 in_=w_raw[g][:].rearrange("p d (q t i) -> p d t q i", t=SLOTS, i=4),
             )
 
-        for quad in range(4):
-            load_scale_rows(ws_raw, ws_hbm, quad)
+        load_scales(ws_raw, ws_hbm)
         load_w(0, nc.scalar)
-        load_x(0, nc.scalar)
+        nc.scalar.dma_start(out=x_first[0][:].bitcast(I32), in_=x_hbm[:, 0, :BANK])
         nc.vector.memset(xs_first[:].bitcast(I32), 0)
-        for quad in range(4):
-            load_scale_rows(xs_first, xs_hbm[:, :, : BANK // 4], quad)
+        load_scales(xs_first, xs_hbm[:, :, : BANK // 4])
+        for d in range(1, D_PASSES):
+            nc.sync.dma_start(out=x_first[d][:].bitcast(I32), in_=x_hbm[:, d, :BANK])
         for g in range(F_PASSES):
             nc.vector.memset(ws_plane[g][:].bitcast(I32), 0)
         nc.vector.memset(xs_rest[:].bitcast(I32), 0)
@@ -115,75 +144,86 @@ def tile_relaxed_document_hash_codes_h2_kernel(
         load_w(1, nc.sync)
         for g in range(F_PASSES):
             nc.sync.dma_start(
-                out=gain_rows[g * SLOTS : (g + 1) * SLOTS, :].rearrange("t (q r) -> t q r", r=8),
-                in_=hidden_scale[g * 512 : (g + 1) * 512].rearrange("(q t r) -> t q r", t=SLOTS, r=8),
+                out=gain_rows[g * SLOTS : (g + 1) * SLOTS, :].rearrange("t (q r) -> t q r", r=RUN),
+                in_=hidden_scale[g * PASS : (g + 1) * PASS].rearrange("(q t r) -> t q r", t=SLOTS, r=RUN),
             )
-        for quad in range(4):
-            load_scale_rows(xs_rest, xs_hbm[:, :, BANK // 4 :], quad)
-        load_x(1, nc.sync)
-        load_code_matrix(0)
-        load_code_matrix(1)
-        load_x(2, nc.sync)
-        load_x(3, nc.sync)
+        load_scales(xs_rest, xs_hbm[:, :, BANK // 4 :])
+        load_x(1)
+        for g in range(F_PASSES):
+            load_code_matrix(g)
         nc.sync.dma_start(out=margin[:], in_=bit_margin.rearrange("(p t) -> p t", t=SLOTS))
         nc.sync.dma_start(out=weight[:], in_=bit_weight.rearrange("(p t) -> p t", t=SLOTS))
+        for c in range(2, CHUNKS):
+            load_x(c)
 
         order_w(0)
-        nc.vector.tensor_copy(out=gain_square[0 : F_PASSES * SLOTS, :], in_=gain_rows[:])
+        nc.vector.tensor_copy(out=gain_square[: F_PASSES * SLOTS, :], in_=gain_rows[:])
         order_w(1)
 
-        def x_scale_cols(c, d):
+        def encoder_pass(sums, c, g, t, d):
             if c == 0:
-                return xs_first[:, d, :]
-            return xs_rest[:, d, (c - 1) * BANK : c * BANK]
-
-        def quantize_h(k):
-            nc.vector.quantize_mx(out=h_codes[k][:].bitcast(FP8X4), scales=h_scales[k][:], in_=h_words[k][:].rearrange("p m t -> p (m t)"))
-
-        def interleave_code_matrix(g, t):
-            nc.scalar.copy(
-                out=c_words[g][:, t * P : (t + 1) * P, :],
-                in_=c_raw[g][:].rearrange("p j (m t) -> p t m j", t=SLOTS)[:, t],
+                codes, scales = x_first[d][:], xs_first[:, d, :]
+            else:
+                codes, scales = x_rest[c - 1][:, d, :], xs_rest[:, d, (c - 1) * BANK : c * BANK]
+            nc.tensor.matmul_mx(
+                out=sums[:],
+                lhsT=w_codes[g][:, d, 2 * t * P : 2 * (t + 1) * P].bitcast(FP4X4),
+                lhsT_scale=ws_plane[g][:, d, t * P : (t + 1) * P],
+                rhs=codes.bitcast(FP8X4),
+                rhs_scale=scales,
+                start=(d == 0),
+                stop=(d == D_PASSES - 1),
             )
 
-        pieces = [(2, 1), (3, 1), (4, 1), (5, 1)]
+        def turn_gain():
+            turned = turn_bank()
+            nc.tensor.transpose(turned[:, :P], gain_square[:], ident[:])
+            nc.vector.tensor_copy(out=gain[:], in_=turned[:, : F_PASSES * SLOTS])
+
+        def code_matrix_views(g):
+            return (
+                c_words[g][:].rearrange("p (t b) j -> p t b j", t=SLOTS),
+                c_raw[g][:].rearrange("p j (b t) -> p t b j", t=SLOTS),
+            )
+
+        def code_matrix_on_vector():
+            target, source = code_matrix_views(0)
+            nc.vector.tensor_copy(out=target, in_=source)
+
+        def code_matrix_on_scalar(t):
+            target, source = code_matrix_views(1)
+            nc.scalar.copy(out=target[:, t], in_=source[:, t])
+
+        vector_extras = {
+            0: turn_gain,
+            1: code_matrix_on_vector,
+            2: lambda: quantize(c_codes[0][:], c_scales[0][:], c_words[0][:]),
+            3: lambda: nc.vector.reciprocal(out=inv_weight[:], in_=weight[:]),
+            4: lambda: nc.vector.tensor_tensor(out=offset[:], in0=margin[:], in1=inv_weight[:], op=ALU.mult),
+            6: lambda: quantize(c_codes[1][:], c_scales[1][:], c_words[1][:]),
+        }
+        scalar_quarters = range(2, 2 + SLOTS)
+
         h_words = {}
-        steps = CHUNKS * F_PASSES
-        for k in range(steps):
+        for k in range(STEPS):
             c, g = divmod(k, F_PASSES)
-            tanh = work.tile([P, SLOTS, BANK], F32, name="tanh", tag="tanh", bufs=3, align_bytes=64)
-            for t in range(SLOTS):
-                acc = psum.tile([P, BANK], F32, name="acc", tag="acc", bufs=ACC_BANKS)
-                for d in range(D_PASSES):
-                    nc.tensor.matmul_mx(
-                        out=acc[:],
-                        lhsT=w_codes[g][:, d, t * 256 : (t + 1) * 256].bitcast(FP4X4),
-                        lhsT_scale=ws_plane[g][:, d, t * P : (t + 1) * P],
-                        rhs=x_codes[c][:, d, :].bitcast(FP8X4),
-                        rhs_scale=x_scale_cols(c, d),
-                        start=(d == 0),
-                        stop=(d == D_PASSES - 1),
-                    )
-                nc.scalar.activation(out=tanh[:, t, :], in_=acc[:], func=ACT.Tanh)
-                if (k, t) in pieces:
-                    interleave_code_matrix(1, pieces.index((k, t)))
+            tanh = streamed("tanh", [P, SLOTS, BANK], F32, 3)
             if k == 0:
-                turned = psum.tile([P, BANK], F32, name="turned", tag="turned", bufs=TURN_BANKS)
-                nc.tensor.transpose(turned[:, 0:P], gain_square[:], ident[:])
-                nc.vector.tensor_copy(out=gain[:], in_=turned[:, 0 : F_PASSES * SLOTS])
-            if k in (2, 6):
-                cg = (2, 6).index(k)
-                nc.vector.quantize_mx(out=c_codes[cg][:].bitcast(FP8X4), scales=c_scales[cg][:], in_=c_words[cg][:].rearrange("p n t -> p (n t)"))
-            if k == 1:
-                nc.vector.tensor_copy(
-                    out=c_words[0][:].rearrange("p (t m) j -> p t m j", t=SLOTS),
-                    in_=c_raw[0][:].rearrange("p j (m t) -> p t m j", t=SLOTS),
-                )
-            if k == 3:
-                nc.vector.reciprocal(out=inv_weight[:], in_=weight[:])
-            if k == 4:
-                nc.vector.tensor_tensor(out=offset[:], in0=margin[:], in1=inv_weight[:], op=ALU.mult)
-            h_words[k] = work.tile([P, BANK, SLOTS], BF16, name="h_words", tag="h_words", bufs=3, align_bytes=64)
+                order = [(t, d) for d in range(D_PASSES) for t in range(SLOTS)]
+            else:
+                order = [(t, d) for t in range(SLOTS) for d in range(D_PASSES)]
+            sums = {}
+            for t, d in order:
+                if d == 0:
+                    sums[t] = sum_bank()
+                encoder_pass(sums[t], c, g, t, d)
+                if d == D_PASSES - 1:
+                    nc.scalar.activation(out=tanh[:, t, :], in_=sums[t][:], func=ACT.Tanh)
+                    if t == 1 and k in scalar_quarters:
+                        code_matrix_on_scalar(scalar_quarters.index(k))
+            if k in vector_extras:
+                vector_extras[k]()
+            h_words[k] = streamed("h_words", [P, BANK, SLOTS], BF16, 3)
             nc.vector.tensor_tensor(
                 out=h_words[k][:].rearrange("p (a i) t -> p a t i", i=4),
                 in0=tanh[:].rearrange("p t (a i) -> p a t i", i=4),
@@ -191,172 +231,121 @@ def tile_relaxed_document_hash_codes_h2_kernel(
                 op=ALU.mult,
             )
             if k > 0:
-                quantize_h(k - 1)
-        quantize_h(steps - 1)
+                quantize(h_codes[k - 1][:], h_scales[k - 1][:], h_words[k - 1][:])
+        quantize(h_codes[STEPS - 1][:], h_scales[STEPS - 1][:], h_words[STEPS - 1][:])
 
-        firsts = [sum(WIDTHS[:i]) for i in range(len(WIDTHS))]
-        banks = [(i, j) for i, width in enumerate(WIDTHS) for j in range(width // P)]
-        last = len(WIDTHS) - 1
-        z, mag, root, square, y, y_words, turned_out = {}, {}, {}, {}, {}, {}, {}
-        codes_hbm = out_1[0].rearrange("p m t -> p (m t)").bitcast(I32)
-        scales_hbm = out_2[0].bitcast(I32)
+        z, mag, root, part, y, y_words, turned_rows = {}, {}, {}, {}, {}, {}, {}
 
-        def slots_of(b):
-            i, j = banks[b]
-            count = BANK // WIDTHS[i]
-            return range(j * count, (j + 1) * count)
+        def halves(b):
+            return [(2 * (b % 2) + n, slice(n * TILE, (n + 1) * TILE)) for n in range(2)]
 
-        def y_part(b):
-            slots = slots_of(b)
-            return y[banks[b][0]][:, slots.start : slots.stop, :].rearrange("p t m -> p (t m)")
+        def y_of(b):
+            return y[b // 2][:, 2 * (b % 2) : 2 * (b % 2) + 2, :].rearrange("p t m -> p (t m)")
 
         def logits(b):
-            i = banks[b][0]
-            width = WIDTHS[i]
-            c, col = divmod(firsts[i], BANK)
-            z[b] = psum.tile([P, BANK], F32, name="acc", tag="acc", bufs=ACC_BANKS)
-            for n, t in enumerate(slots_of(b)):
+            c, first = divmod(b // 2 * TILE, BANK)
+            docs = slice(first, first + TILE)
+            z[b] = sum_bank()
+            for t, cols in halves(b):
                 for g in range(F_PASSES):
                     k = c * F_PASSES + g
                     nc.tensor.matmul_mx(
-                        out=z[b][:, n * width : (n + 1) * width],
+                        out=z[b][:, cols],
                         lhsT=c_codes[g][:, t * P : (t + 1) * P].bitcast(FP8X4),
                         lhsT_scale=c_scales[g][:, t * P : (t + 1) * P],
-                        rhs=h_codes[k][:, col : col + width].bitcast(FP8X4),
-                        rhs_scale=h_scales[k][:, col : col + width],
+                        rhs=h_codes[k][:, docs].bitcast(FP8X4),
+                        rhs_scale=h_scales[k][:, docs],
                         start=(g == 0),
                         stop=(g == F_PASSES - 1),
                     )
 
         def magnitude(b):
-            mag[b] = work.tile([P, BANK], F32, name="mag", tag="mag", bufs=3, align_bytes=64)
+            mag[b] = streamed("mag", [P, BANK], F32, 3)
             nc.scalar.activation(out=mag[b][:], in_=z[b][:], func=ACT.Abs)
 
         def inverse_root(b):
-            width = WIDTHS[banks[b][0]]
-            root[b] = work.tile([P, BANK], F32, name="root", tag="root", bufs=5, align_bytes=64)
-            for n, t in enumerate(slots_of(b)):
-                cols = slice(n * width, (n + 1) * width)
+            root[b] = streamed("root", [P, BANK], F32, 5)
+            for t, cols in halves(b):
                 nc.scalar.activation(
                     out=root[b][:, cols], in_=mag[b][:, cols], func=ACT.Abs_reciprocal_sqrt,
                     scale=inv_weight[:, t : t + 1], bias=offset[:, t : t + 1],
                 )
 
-        def square_root(b):
-            square[b] = work.tile([P, BANK], F32, name="square", tag="square", bufs=5, align_bytes=64)
-            if b in POOL_SQUARES:
-                nc.gpsimd.tensor_tensor(out=square[b][:], in0=root[b][:], in1=root[b][:], op=ALU.mult)
-            elif b not in VECTOR_SQUARES:
-                nc.scalar.activation(out=square[b][:], in_=root[b][:], func=ACT.Square)
-
-        def product(b):
-            i, j = banks[b]
-            if j == 0:
-                y[i] = work.tile([P, SLOTS, WIDTHS[i]], F32, name="y", tag="y", bufs=4, align_bytes=64)
-            if b in VECTOR_SQUARES:
-                nc.vector.tensor_tensor(out=square[b][:], in0=z[b][:], in1=root[b][:], op=ALU.mult)
+        def first_product(b):
+            part[b] = streamed("part", [P, BANK], F32, 5)
+            if b < VECTOR_SQUARES:
+                nc.vector.tensor_tensor(out=part[b][:], in0=z[b][:], in1=root[b][:], op=ALU.mult)
             else:
-                nc.vector.tensor_tensor(out=y_part(b), in0=z[b][:], in1=square[b][:], op=ALU.mult)
+                nc.scalar.activation(out=part[b][:], in_=root[b][:], func=ACT.Square)
 
         def second_product(b):
-            if b in VECTOR_SQUARES:
-                nc.vector.tensor_tensor(out=y_part(b), in0=square[b][:], in1=root[b][:], op=ALU.mult)
+            other = root[b] if b < VECTOR_SQUARES else z[b]
+            nc.vector.tensor_tensor(out=y_of(b), in0=other[:], in1=part[b][:], op=ALU.mult)
 
         def round_y(i):
-            y_words[i] = work.tile([P, WIDTHS[i], SLOTS], BF16, name="y_words", tag="y_words", bufs=4, align_bytes=64)
-            if i < last:
-                nc.gpsimd.tensor_scalar(
-                    out=y_words[i][:], in0=y[i][:].rearrange("p t m -> p m t"),
-                    scalar1=1.0, scalar2=-0.0, op0=ALU.mult, op1=ALU.add,
-                )
-            else:
-                nc.vector.tensor_copy(
-                    out=y_words[i][:].rearrange("p (a i) t -> p a t i", i=4),
-                    in_=y[i][:].rearrange("p t (a i) -> p a t i", i=4),
-                )
+            y_words[i] = streamed("y_words", [P, TILE, SLOTS], BF16, 4)
+            nc.vector.tensor_copy(
+                out=y_words[i][:].rearrange("p (a i) t -> p a t i", i=4),
+                in_=y[i][:].rearrange("p t (a i) -> p a t i", i=4),
+            )
 
         def quantize_y(i):
-            cols = slice(firsts[i], firsts[i] + WIDTHS[i])
-            nc.vector.quantize_mx(out=y_codes[:, cols].bitcast(FP8X4), scales=y_scales[:, cols], in_=y_words[i][:].rearrange("p m t -> p (m t)"))
+            end = (i + 1) * TILE
+            quantize(y_codes[:, end - TILE : end], y_scales[:, end - TILE : end], y_words[i][:])
+            nc.sync.dma_start(out=codes_hbm[:, end - TILE : end], in_=y_codes[:, end - TILE : end].bitcast(I32))
+            if end % (M // 2) == 0:
+                words = slice((end - M // 2) // 4, end // 4)
+                for quad in range(QUADS):
+                    nc.sync.dma_start(
+                        out=scales_hbm[4 * quad : 4 * quad + 4, words],
+                        in_=y_scales[scale_rows(quad), :].bitcast(I32)[:, words],
+                    )
 
-            end = cols.stop
-            if end % BANK == 0:
-                nc.sync.dma_start(out=codes_hbm[:, end - BANK : end], in_=y_codes[:, end - BANK : end].bitcast(I32))
-            if end == 1024:
-                store_scales(0, end)
-            if end == M:
-                store_scales(1024, M)
-
-        def store_scales(first, end):
-            cols = slice(first // 4, end // 4)
-            for quad in range(4):
-                nc.sync.dma_start(
-                    out=scales_hbm[4 * quad : 4 * quad + 4, cols],
-                    in_=y_scales[32 * quad : 32 * quad + 4, :].bitcast(I32)[:, cols],
-                )
-
-        def turn(b):
-            i, j = banks[b]
-            turned_out[b] = psum.tile([P, BANK], F32, name="turned", tag="turned", bufs=TURN_BANKS)
+        def turn(r):
+            turned_rows[r] = turn_bank()
+            docs = slice(r % 2 * P, (r % 2 + 1) * P)
             for t in range(SLOTS):
-                nc.tensor.transpose(turned_out[b][:, t * P : (t + 1) * P], y[i][:, t, j * P : (j + 1) * P], ident[:])
+                nc.tensor.transpose(turned_rows[r][:, t * P : (t + 1) * P], y[r // 2][:, t, docs], ident[:])
 
-        def copy_out(b):
-            rows = work.tile([P, N], F32, name="rows", tag="rows", bufs=6, align_bytes=64)
-            target = rows[:].rearrange("p (n t) -> p n t", t=SLOTS)
-            source = turned_out[b][:].rearrange("p (t n) -> p n t", t=SLOTS)
-            if b in SCALAR_COPIES:
+        def copy_out(r):
+            rows = streamed("rows", [P, N], F32, 6)
+            target = rows[:].rearrange("m (p t) -> m p t", t=SLOTS)
+            source = turned_rows[r][:].rearrange("m (t p) -> m p t", t=SLOTS)
+            if r >= M // P - SCALAR_COPIES:
                 nc.scalar.copy(out=target, in_=source)
             else:
                 nc.vector.tensor_copy(out=target, in_=source)
-            nc.sync.dma_start(out=out_0[b * P : (b + 1) * P, :], in_=rows[:])
+            nc.sync.dma_start(out=out_0[r * P : (r + 1) * P, :], in_=rows[:])
 
-        for b in range(ACC_BANKS):
+        for b in range(SUM_BANKS):
             logits(b)
-        to_turn, to_copy, to_quantize = [], [], []
-
-        def turn_ready():
-            while to_turn and len(to_copy) < TURN_BANKS:
-                turn(to_turn[0])
-                to_copy.append(to_turn[0])
-                to_turn.remove(to_turn[0])
-
-        def copy_next():
-            copy_out(to_copy[0])
-            to_copy.remove(to_copy[0])
-            turn_ready()
-
-        for tick in range(len(banks) + LAG):
-            if tick < len(banks):
+        for tick in range(PAIRS + LAG):
+            if tick < PAIRS:
                 magnitude(tick)
-            if 1 <= tick <= len(banks):
+            if 1 <= tick <= PAIRS:
                 inverse_root(tick - 1)
-                if tick - 1 in POOL_SQUARES:
-                    square_root(tick - 1)
-            if 2 <= tick < len(banks) + 2 and tick - 2 not in POOL_SQUARES:
-                square_root(tick - 2)
             if tick < LAG:
                 continue
             b = tick - LAG
-            i, j = banks[b]
-            finishes = j == WIDTHS[i] // P - 1
-            if finishes and i >= 2 and b not in VECTOR_SQUARES:
-                quantize_y(i - 2)
-            product(b)
-            if b + ACC_BANKS < len(banks):
-                logits(b + ACC_BANKS)
-            if to_copy:
-                copy_next()
-            if finishes and i >= 2 and b in VECTOR_SQUARES:
-                quantize_y(i - 2)
-            second_product(b)
-            if finishes:
-                if i == last:
-                    for done in range(last - 2 + 1, last):
-                        quantize_y(done)
+            i = b // 2
+            if b % 2 == 0:
+                y[i] = streamed("y", [P, SLOTS, TILE], F32, 4)
+            first_product(b)
+            if b >= VECTOR_SQUARES:
+                second_product(b)
+            if b + SUM_BANKS < PAIRS:
+                logits(b + SUM_BANKS)
+            if i > 0:
+                copy_out(b - 2)
+            if b % 2 == 1:
+                if b < VECTOR_SQUARES:
+                    second_product(b - 1)
+                    second_product(b)
+                if i > 0:
+                    quantize_y(i - 1)
                 round_y(i)
-                to_turn.extend(range(b - j, b + 1))
-                turn_ready()
-        while to_copy:
-            copy_next()
-        quantize_y(last)
+                turn(b - 1)
+                turn(b)
+        copy_out(PAIRS - 2)
+        copy_out(PAIRS - 1)
+        quantize_y(TILES - 1)

from contextlib import ExitStack

import concourse.mybir as mybir
from concourse.masks import make_identity

M, D, F, N = 2048, 1536, 1024, 512
FLOPS = 2 * M * D * F + 2 * M * F * N

F32 = mybir.dt.float32
BF16 = mybir.dt.bfloat16
I32 = mybir.dt.int32
U32 = mybir.dt.uint32
U8 = mybir.dt.uint8
FP8X4 = mybir.dt.float8_e4m3fn_x4
FP4X4 = mybir.dt.float4_e2m1fn_x4
ACT = mybir.ActivationFunctionType
ALU = mybir.AluOpType

P = 128
SLOTS = 4
PASS = P * SLOTS
BANK = 512
QUADS = 4
RUN = 8
D_PASSES = D // PASS
F_PASSES = F // PASS
CHUNKS = M // BANK
STEPS = CHUNKS * F_PASSES
TILE = 256
TILES = M // TILE
PAIRS = 2 * TILES

SUM_BANKS = 6
TURN_BANKS = 2
VECTOR_SQUARES = 4
SCALAR_COPIES = 4
LAG = 2


def tile_relaxed_document_hash_codes_h2_kernel(
    tc, x_words, x_scales, w_words, w_scales, hidden_scale, code_matrix, bit_margin, bit_weight,
    out_0, out_1, out_2,
):
    nc = tc.nc
    with ExitStack() as ctx:
        keep = ctx.enter_context(tc.tile_pool(name="keep", bufs=1))
        work = ctx.enter_context(tc.tile_pool(name="work", bufs=3))
        psum = ctx.enter_context(tc.psum_pool(name="psum", bufs=1))
        ctx.enter_context(tc.manual_schedule())

        def kept(name, shape, dtype):
            return keep.tile(shape, dtype, name=name, align_bytes=64)

        def streamed(name, shape, dtype, bufs):
            return work.tile(shape, dtype, name=name, tag=name, bufs=bufs, align_bytes=64)

        def sum_bank():
            return psum.tile([P, BANK], F32, name="sums", tag="sums", bufs=SUM_BANKS)

        def turn_bank():
            return psum.tile([P, BANK], F32, name="turned", tag="turned", bufs=TURN_BANKS)

        def quantize(codes, scales, words):
            nc.vector.quantize_mx(
                out=codes.bitcast(FP8X4), scales=scales, in_=words.rearrange("p c t -> p (c t)")
            )

        x_hbm = x_words.rearrange("d p m t -> p d (m t)").bitcast(I32)
        xs_hbm = x_scales.rearrange("d r m -> r d m").bitcast(I32)
        w_hbm = w_words.rearrange("d p b -> p d b").bitcast(I32)
        ws_hbm = w_scales.rearrange("d r f -> r d f").bitcast(I32)
        codes_hbm = out_1[0].rearrange("p m t -> p (m t)").bitcast(I32)
        scales_hbm = out_2[0].bitcast(I32)

        x_first = [kept("x_first%d" % d, [P, BANK], U32) for d in range(D_PASSES)]
        x_rest = [kept("x_rest%d" % c, [P, D_PASSES, BANK], U32) for c in range(1, CHUNKS)]
        xs_first = kept("xs_first", [P, D_PASSES, BANK], U8)
        xs_rest = kept("xs_rest", [P, D_PASSES, M - BANK], U8)
        w_raw = [kept("w_raw%d" % g, [P, D_PASSES, PASS // 2], I32) for g in range(F_PASSES)]
        w_codes = [kept("w_codes%d" % g, [P, D_PASSES, 2 * PASS], U8) for g in range(F_PASSES)]
        ws_raw = kept("ws_raw", [P, D_PASSES, F], U8)
        ws_plane = [kept("ws_plane%d" % g, [P, D_PASSES, PASS], U8) for g in range(F_PASSES)]
        gain_rows = kept("gain_rows", [F_PASSES * SLOTS, P], BF16)
        gain_square = kept("gain_square", [P, P], F32)
        gain = kept("gain", [P, F_PASSES * SLOTS], F32)
        ident = kept("ident", [P, P], F32)
        c_raw = [kept("c_raw%d" % g, [P, SLOTS, N], BF16) for g in range(F_PASSES)]
        c_words = [kept("c_words%d" % g, [P, N, SLOTS], BF16) for g in range(F_PASSES)]
        c_codes = [kept("c_codes%d" % g, [P, N], U32) for g in range(F_PASSES)]
        c_scales = [kept("c_scales%d" % g, [P, N], U8) for g in range(F_PASSES)]
        h_codes = [kept("h_codes%d" % k, [P, BANK], U32) for k in range(STEPS)]
        h_scales = [kept("h_scales%d" % k, [P, BANK], U8) for k in range(STEPS)]
        margin = kept("margin", [P, SLOTS], BF16)
        weight = kept("weight", [P, SLOTS], BF16)
        inv_weight = kept("inv_weight", [P, SLOTS], F32)
        offset = kept("offset", [P, SLOTS], F32)
        y_codes = kept("y_codes", [P, M], U32)
        y_scales = kept("y_scales", [P, M], U8)

        def scale_rows(quad):
            return slice(32 * quad, 32 * quad + 4)

        def load_scales(plane, hbm):
            for quad in range(QUADS):
                nc.sync.dma_start(out=plane[scale_rows(quad)].bitcast(I32), in_=hbm[4 * quad : 4 * quad + 4])

        def load_w(g, queue):
            queue.dma_start(out=w_raw[g][:], in_=w_hbm[:, :, g * PASS // 2 : (g + 1) * PASS // 2])

        def load_x(c):
            nc.sync.dma_start(out=x_rest[c - 1][:].bitcast(I32), in_=x_hbm[:, :, c * BANK : (c + 1) * BANK])

        def load_code_matrix(g):
            rows = code_matrix[g * PASS : (g + 1) * PASS, :].rearrange("(q t r) n -> r q t n", t=SLOTS, r=RUN)
            for r in range(RUN):
                nc.sync.dma_start(out=c_raw[g][r:P:RUN], in_=rows[r])

        def order_w(g):
            for quad in range(QUADS):
                rows = scale_rows(quad)
                nc.vector.tensor_copy(
                    out=ws_plane[g][rows].bitcast(I32).rearrange("p d (t q i) -> p d t q i", t=SLOTS, i=2),
                    in_=ws_raw[rows, :, g * PASS : (g + 1) * PASS]
                    .bitcast(I32)
                    .rearrange("p d (q t i) -> p d t q i", t=SLOTS, i=2),
                )
            nc.vector.tensor_copy(
                out=w_codes[g][:].bitcast(I32).rearrange("p d (t q i) -> p d t q i", t=SLOTS, i=4),
                in_=w_raw[g][:].rearrange("p d (q t i) -> p d t q i", t=SLOTS, i=4),
            )

        load_scales(ws_raw, ws_hbm)
        load_w(0, nc.scalar)
        nc.scalar.dma_start(out=x_first[0][:].bitcast(I32), in_=x_hbm[:, 0, :BANK])
        nc.vector.memset(xs_first[:].bitcast(I32), 0)
        load_scales(xs_first, xs_hbm[:, :, : BANK // 4])
        for d in range(1, D_PASSES):
            nc.sync.dma_start(out=x_first[d][:].bitcast(I32), in_=x_hbm[:, d, :BANK])
        for g in range(F_PASSES):
            nc.vector.memset(ws_plane[g][:].bitcast(I32), 0)
        nc.vector.memset(xs_rest[:].bitcast(I32), 0)
        nc.gpsimd.memset(gain_square[:], 0.0)
        make_identity(nc, ident[:])
        load_w(1, nc.sync)
        for g in range(F_PASSES):
            nc.sync.dma_start(
                out=gain_rows[g * SLOTS : (g + 1) * SLOTS, :].rearrange("t (q r) -> t q r", r=RUN),
                in_=hidden_scale[g * PASS : (g + 1) * PASS].rearrange("(q t r) -> t q r", t=SLOTS, r=RUN),
            )
        load_scales(xs_rest, xs_hbm[:, :, BANK // 4 :])
        load_x(1)
        for g in range(F_PASSES):
            load_code_matrix(g)
        nc.sync.dma_start(out=margin[:], in_=bit_margin.rearrange("(p t) -> p t", t=SLOTS))
        nc.sync.dma_start(out=weight[:], in_=bit_weight.rearrange("(p t) -> p t", t=SLOTS))
        for c in range(2, CHUNKS):
            load_x(c)

        order_w(0)
        nc.vector.tensor_copy(out=gain_square[: F_PASSES * SLOTS, :], in_=gain_rows[:])
        order_w(1)

        def encoder_pass(sums, c, g, t, d):
            if c == 0:
                codes, scales = x_first[d][:], xs_first[:, d, :]
            else:
                codes, scales = x_rest[c - 1][:, d, :], xs_rest[:, d, (c - 1) * BANK : c * BANK]
            nc.tensor.matmul_mx(
                out=sums[:],
                lhsT=w_codes[g][:, d, 2 * t * P : 2 * (t + 1) * P].bitcast(FP4X4),
                lhsT_scale=ws_plane[g][:, d, t * P : (t + 1) * P],
                rhs=codes.bitcast(FP8X4),
                rhs_scale=scales,
                start=(d == 0),
                stop=(d == D_PASSES - 1),
            )

        def turn_gain():
            turned = turn_bank()
            nc.tensor.transpose(turned[:, :P], gain_square[:], ident[:])
            nc.vector.tensor_copy(out=gain[:], in_=turned[:, : F_PASSES * SLOTS])

        def code_matrix_views(g):
            return (
                c_words[g][:].rearrange("p (t b) j -> p t b j", t=SLOTS),
                c_raw[g][:].rearrange("p j (b t) -> p t b j", t=SLOTS),
            )

        def code_matrix_on_vector():
            target, source = code_matrix_views(0)
            nc.vector.tensor_copy(out=target, in_=source)

        def code_matrix_on_scalar(t):
            target, source = code_matrix_views(1)
            nc.scalar.copy(out=target[:, t], in_=source[:, t])

        vector_extras = {
            0: turn_gain,
            1: code_matrix_on_vector,
            2: lambda: quantize(c_codes[0][:], c_scales[0][:], c_words[0][:]),
            3: lambda: nc.vector.reciprocal(out=inv_weight[:], in_=weight[:]),
            4: lambda: nc.vector.tensor_tensor(out=offset[:], in0=margin[:], in1=inv_weight[:], op=ALU.mult),
            6: lambda: quantize(c_codes[1][:], c_scales[1][:], c_words[1][:]),
        }
        scalar_quarters = range(2, 2 + SLOTS)

        h_words = {}
        for k in range(STEPS):
            c, g = divmod(k, F_PASSES)
            tanh = streamed("tanh", [P, SLOTS, BANK], F32, 3)
            if k == 0:
                order = [(t, d) for d in range(D_PASSES) for t in range(SLOTS)]
            else:
                order = [(t, d) for t in range(SLOTS) for d in range(D_PASSES)]
            sums = {}
            for t, d in order:
                if d == 0:
                    sums[t] = sum_bank()
                encoder_pass(sums[t], c, g, t, d)
                if d == D_PASSES - 1:
                    nc.scalar.activation(out=tanh[:, t, :], in_=sums[t][:], func=ACT.Tanh)
                    if t == 1 and k in scalar_quarters:
                        code_matrix_on_scalar(scalar_quarters.index(k))
            if k in vector_extras:
                vector_extras[k]()
            h_words[k] = streamed("h_words", [P, BANK, SLOTS], BF16, 3)
            nc.vector.tensor_tensor(
                out=h_words[k][:].rearrange("p (a i) t -> p a t i", i=4),
                in0=tanh[:].rearrange("p t (a i) -> p a t i", i=4),
                in1=gain[:, g * SLOTS : (g + 1) * SLOTS].unsqueeze(1).unsqueeze(3).to_broadcast([P, BANK // 4, SLOTS, 4]),
                op=ALU.mult,
            )
            if k > 0:
                quantize(h_codes[k - 1][:], h_scales[k - 1][:], h_words[k - 1][:])
        quantize(h_codes[STEPS - 1][:], h_scales[STEPS - 1][:], h_words[STEPS - 1][:])

        z, mag, root, part, y, y_words, turned_rows = {}, {}, {}, {}, {}, {}, {}

        def halves(b):
            return [(2 * (b % 2) + n, slice(n * TILE, (n + 1) * TILE)) for n in range(2)]

        def y_of(b):
            return y[b // 2][:, 2 * (b % 2) : 2 * (b % 2) + 2, :].rearrange("p t m -> p (t m)")

        def logits(b):
            c, first = divmod(b // 2 * TILE, BANK)
            docs = slice(first, first + TILE)
            z[b] = sum_bank()
            for t, cols in halves(b):
                for g in range(F_PASSES):
                    k = c * F_PASSES + g
                    nc.tensor.matmul_mx(
                        out=z[b][:, cols],
                        lhsT=c_codes[g][:, t * P : (t + 1) * P].bitcast(FP8X4),
                        lhsT_scale=c_scales[g][:, t * P : (t + 1) * P],
                        rhs=h_codes[k][:, docs].bitcast(FP8X4),
                        rhs_scale=h_scales[k][:, docs],
                        start=(g == 0),
                        stop=(g == F_PASSES - 1),
                    )

        def magnitude(b):
            mag[b] = streamed("mag", [P, BANK], F32, 3)
            nc.scalar.activation(out=mag[b][:], in_=z[b][:], func=ACT.Abs)

        def inverse_root(b):
            root[b] = streamed("root", [P, BANK], F32, 5)
            for t, cols in halves(b):
                nc.scalar.activation(
                    out=root[b][:, cols], in_=mag[b][:, cols], func=ACT.Abs_reciprocal_sqrt,
                    scale=inv_weight[:, t : t + 1], bias=offset[:, t : t + 1],
                )

        def first_product(b):
            part[b] = streamed("part", [P, BANK], F32, 5)
            if b < VECTOR_SQUARES:
                nc.vector.tensor_tensor(out=part[b][:], in0=z[b][:], in1=root[b][:], op=ALU.mult)
            else:
                nc.scalar.activation(out=part[b][:], in_=root[b][:], func=ACT.Square)

        def second_product(b):
            other = root[b] if b < VECTOR_SQUARES else z[b]
            nc.vector.tensor_tensor(out=y_of(b), in0=other[:], in1=part[b][:], op=ALU.mult)

        def round_y(i):
            y_words[i] = streamed("y_words", [P, TILE, SLOTS], BF16, 4)
            nc.vector.tensor_copy(
                out=y_words[i][:].rearrange("p (a i) t -> p a t i", i=4),
                in_=y[i][:].rearrange("p t (a i) -> p a t i", i=4),
            )

        def quantize_y(i):
            end = (i + 1) * TILE
            quantize(y_codes[:, end - TILE : end], y_scales[:, end - TILE : end], y_words[i][:])
            nc.sync.dma_start(out=codes_hbm[:, end - TILE : end], in_=y_codes[:, end - TILE : end].bitcast(I32))
            if end % (M // 2) == 0:
                words = slice((end - M // 2) // 4, end // 4)
                for quad in range(QUADS):
                    nc.sync.dma_start(
                        out=scales_hbm[4 * quad : 4 * quad + 4, words],
                        in_=y_scales[scale_rows(quad), :].bitcast(I32)[:, words],
                    )

        def turn(r):
            turned_rows[r] = turn_bank()
            docs = slice(r % 2 * P, (r % 2 + 1) * P)
            for t in range(SLOTS):
                nc.tensor.transpose(turned_rows[r][:, t * P : (t + 1) * P], y[r // 2][:, t, docs], ident[:])

        def copy_out(r):
            rows = streamed("rows", [P, N], F32, 6)
            target = rows[:].rearrange("m (p t) -> m p t", t=SLOTS)
            source = turned_rows[r][:].rearrange("m (t p) -> m p t", t=SLOTS)
            if r >= M // P - SCALAR_COPIES:
                nc.scalar.copy(out=target, in_=source)
            else:
                nc.vector.tensor_copy(out=target, in_=source)
            nc.sync.dma_start(out=out_0[r * P : (r + 1) * P, :], in_=rows[:])

        for b in range(SUM_BANKS):
            logits(b)
        for tick in range(PAIRS + LAG):
            if tick < PAIRS:
                magnitude(tick)
            if 1 <= tick <= PAIRS:
                inverse_root(tick - 1)
            if tick < LAG:
                continue
            b = tick - LAG
            i = b // 2
            if b % 2 == 0:
                y[i] = streamed("y", [P, SLOTS, TILE], F32, 4)
            first_product(b)
            if b >= VECTOR_SQUARES:
                second_product(b)
            if b + SUM_BANKS < PAIRS:
                logits(b + SUM_BANKS)
            if i > 0:
                copy_out(b - 2)
            if b % 2 == 1:
                if b < VECTOR_SQUARES:
                    second_product(b - 1)
                    second_product(b)
                if i > 0:
                    quantize_y(i - 1)
                round_y(i)
                turn(b - 1)
                turn(b)
        copy_out(PAIRS - 2)
        copy_out(PAIRS - 1)
        quantize_y(TILES - 1)
